import numpy as np
import ml_dtypes


def mxq(x, axis, fmt="e4m3"):
    dtype, down = {"e4m3": (ml_dtypes.float8_e4m3fn, 7), "e5m2": (ml_dtypes.float8_e5m2, 14)}[fmt]
    v = np.moveaxis(np.asarray(x, np.float32).astype(ml_dtypes.bfloat16).astype(np.float64), axis, -1)
    blocks = v.reshape(v.shape[:-1] + (-1, 32))
    amax = np.abs(blocks).max(-1, keepdims=True)
    byte = np.maximum(np.where(amax > 0, np.frexp(amax)[1] - 1 + 127, 0) - down, 1)
    scale = np.exp2(byte - 127.0)
    codes = (blocks / scale).astype(np.float32).astype(dtype).astype(np.float64)
    return np.moveaxis((codes * scale).reshape(v.shape), -1, axis)


WIDE = False


def mx_kscale(k):
    if not WIDE:
        return np.ones(k)
    levels = np.array([10, -10, 5, -5, 0])
    if k % 512:
        return np.exp2(np.random.permutation(np.resize(levels, k // 32))).repeat(32)
    a = np.empty((k // 512, 16))
    for p in range(k // 512):
        a[p, :8] = np.random.permutation(np.resize(levels, 8))
        for g in range(8):
            far = levels[np.abs(levels - a[p, g]) >= 10]
            a[p, g + 8] = far[np.random.randint(len(far))]
    return np.exp2(a.ravel()).repeat(32)


def f64(x):
    return np.asarray(x).astype(np.float64)


def striped(idx):
    return np.tile(idx.reshape(-1, 16).T, (8, 1)).astype(np.uint16)


def unstriped(offs):
    return offs[:16].T.reshape(-1).astype(np.int64)


def pack_weight(w):
    k, n = w.shape
    w = f64(np.asarray(w, np.float32).astype(ml_dtypes.bfloat16)).reshape(k // 32, 32, n)
    amax = np.abs(w).max(1)
    byte = np.clip(np.where(amax > 0, np.frexp(amax)[1] - 1 + 127 - 7, 1), 1, 254)
    scaled = (w * np.exp2(127.0 - byte)[:, None, :]).reshape(k, n).astype(np.float32)
    words = np.ascontiguousarray(scaled.reshape(k // 512, 128, 4, n).transpose(0, 1, 3, 2)).astype(ml_dtypes.float8_e4m3fn).view(np.uint8)
    return words, np.ascontiguousarray(byte.astype(np.uint8).reshape(k // 512, 16, n))


def unpack_weight(words, scales):
    g, p, n, _ = words.shape
    vals = np.ascontiguousarray(words).view(ml_dtypes.float8_e4m3fn).astype(np.float64) * np.repeat(np.exp2(scales.astype(np.float64) - 127.0), 8, axis=1)[..., None]
    return vals.transpose(0, 1, 3, 2).reshape(g * 512, n)


K, T, S, N, D, U, V, W = 1024, 2048, 512, 128, 4, 1024, 256, 256


def setup_inputs():
    n = np.random.standard_normal
    s = mx_kscale(K)[:, None]
    packed_xT = pack_weight(n((K, T)) * s)
    return {
        "x_words": packed_xT[0],
        "x_scales": packed_xT[1],
        "w1": (n((K, N)) / np.sqrt(K) / s).astype(np.float32),
        "rule": (n((N, U)) * 0.5 - 1.0).astype(np.float32),
        "offs": striped(np.random.permutation(T)[:S]),
        "la": striped(np.random.permutation(np.concatenate([np.arange(S), np.random.randint(0, S, U - S)]))),
        "ra": striped(np.random.permutation(np.concatenate([np.arange(S), np.random.randint(0, S, U - S)]))),
        "lb": striped(np.random.randint(0, V, W)),
        "rb": striped(np.random.randint(0, S, W)),
    }


def reference(x_words, x_scales, w1, rule, offs, la, ra, lb, rb):
    xq = unpack_weight(x_words, x_scales)[:, unstriped(offs)]
    y = mxq(f64(w1), 0, "e4m3").T @ xq
    cand = y[:, unstriped(la)] + y[:, unstriped(ra)] + f64(rule)
    top = cand.reshape(len(cand), -1, D).max(axis=2)
    cand2 = top[:, unstriped(lb)] + y[:, unstriped(rb)]
    top2 = cand2.reshape(len(cand2), -1, D).max(axis=2)
    return top2 - (0.5 * (cand2.reshape(len(cand2), -1, D).mean(axis=2)))

@@ -1,0 +1,184 @@
+from contextlib import ExitStack
+
+import concourse.mybir as mybir
+
+K, T, S, N, D, U, V, W = 1024, 2048, 512, 128, 4, 1024, 256, 256
+FLOPS = 2 * K * N * S
+
+F32 = mybir.dt.float32
+BF16 = mybir.dt.bfloat16
+I32 = mybir.dt.int32
+U32 = mybir.dt.uint32
+U16 = mybir.dt.uint16
+U8 = mybir.dt.uint8
+FP8X4 = mybir.dt.float8_e4m3fn_x4
+ALU = mybir.AluOpType
+COPY = mybir.ActivationFunctionType.Copy
+AX = mybir.AxisListType.X
+
+P = 128
+PACK = 4
+PASSES = K // (P * PACK)
+PIECES = ((0, 256), (256, 384), (384, 512))
+CHUNK = 256
+
+
+def entries(offsets, lo, hi):
+    return offsets[:, lo // 16 : hi // 16]
+
+
+def tile_picked_ycky_vit_p_kernel(
+    tc, x_words, x_scales, w1, rule, offs, la, ra, lb, rb, out
+):
+    nc = tc.nc
+    with ExitStack() as ctx:
+        sb = ctx.enter_context(tc.tile_pool(name="sb", bufs=1))
+        ps = ctx.enter_context(tc.psum_pool(name="ps", bufs=1))
+
+        offs_t = sb.tile([P, S // 16], U16, name="offs_t")
+        la_t = sb.tile([P, U // 16], U16, name="la_t")
+        ra_t = sb.tile([P, U // 16], U16, name="ra_t")
+        lb_t = sb.tile([P, W // 16], U16, name="lb_t")
+        rb_t = sb.tile([P, W // 16], U16, name="rb_t")
+
+        w_raw = sb.tile([P, PASSES, PACK, N], F32, name="w_raw")
+        words = [sb.tile([P, T], I32, name=f"words{o}", align_bytes=64) for o in range(PASSES)]
+        scales = sb.tile([P, T], U8, name="scales")
+        rule_t = sb.tile([P, U], F32, name="rule_t")
+
+        nc.vector.memset(scales[:].bitcast(I32), 0)
+        for q in range(4):
+            nc.gpsimd.dma_start(
+                scales[32 * q : 32 * q + 4 * PASSES, :].bitcast(I32),
+                x_scales[:, 4 * q : 4 * q + 4, :].bitcast(I32),
+            )
+        nc.sync.dma_start(w_raw[:], w1.rearrange("(o p j) m -> p o j m", o=PASSES, j=PACK))
+        nc.sync.dma_start(offs_t[:], offs)
+        for o in range(PASSES):
+            nc.sync.dma_start(words[o][:], x_words[o].rearrange("p n t -> p (n t)").bitcast(I32))
+        nc.sync.dma_start(la_t[:], la)
+        nc.sync.dma_start(ra_t[:], ra)
+        nc.sync.dma_start(rule_t[:], rule)
+        nc.sync.dma_start(rb_t[:], rb)
+        nc.sync.dma_start(lb_t[:], lb)
+
+        w_bf = sb.tile([P, PASSES, N, PACK], BF16, name="w_bf", align_bytes=64)
+        nc.scalar.activation(w_bf[:], w_raw[:].rearrange("p o j m -> p o m j"), COPY)
+        w_codes = sb.tile([P, PASSES * N], U32, name="w_codes", align_bytes=64)
+        w_scales = sb.tile([P, PASSES * N], U8, name="w_scales", align_bytes=64)
+        nc.vector.quantize_mx(
+            out=w_codes[:].bitcast(FP8X4),
+            scales=w_scales[:],
+            in_=w_bf[:].rearrange("p o m j -> p (o m j)"),
+        )
+
+        picked = [sb.tile([P, S], U32, name=f"picked{o}", align_bytes=64) for o in range(PASSES)]
+        nc.vector.tensor_copy(picked[0][:], words[0][:].bitcast(U32).indirect(offs_t[:]))
+        picked_scales = sb.tile([P, S], U8, name="picked_scales", tag="words0", align_bytes=64)
+        nc.vector.tensor_copy(picked_scales[:], scales[:].indirect(offs_t[:]))
+
+        banks = [ps.tile([P, hi - lo], F32, name=f"bank{lo}") for lo, hi in PIECES]
+
+        def product(bank, o, lo, hi):
+            nc.tensor.matmul_mx(
+                out=bank[:],
+                lhsT=w_codes[:, o * N : (o + 1) * N].bitcast(FP8X4),
+                lhsT_scale=w_scales[:, o * N : (o + 1) * N],
+                rhs=picked[o][:, lo:hi].bitcast(FP8X4),
+                rhs_scale=picked_scales[4 * o : P, lo:hi],
+                start=(o == 0),
+                stop=(o == PASSES - 1),
+            )
+
+        for bank, (lo, hi) in zip(banks, PIECES):
+            product(bank, 0, lo, hi)
+        y = sb.tile([P, S], F32, name="y")
+        for lo, hi in PIECES:
+            nc.vector.tensor_copy(
+                picked[1][:, lo:hi], words[1][:].bitcast(U32).indirect(entries(offs_t, lo, hi))
+            )
+        for bank, (lo, hi) in zip(banks, PIECES):
+            product(bank, 1, lo, hi)
+            if hi < S:
+                nc.scalar.activation(y[:, lo:hi], bank[:], COPY)
+            else:
+                nc.vector.tensor_copy(y[:, lo:hi], bank[:])
+
+        left = sb.tile([P, U], F32, name="left")
+        right = sb.tile([P, U], F32, name="right")
+        part = sb.tile([P, U], F32, name="part")
+        cand = sb.tile([P, U], F32, name="cand")
+        top = sb.tile([P, V], F32, name="top")
+
+        def cols(c):
+            return slice(c[0], c[1])
+
+        def fetch(dst, offsets, c):
+            nc.scalar.activation(
+                dst[:, cols(c)], y[:].indirect(entries(offsets, c[0], c[1])), COPY
+            )
+
+        def fetch_add(c):
+            nc.vector.tensor_tensor(
+                part[:, cols(c)],
+                y[:].indirect(entries(ra_t, c[0], c[1])),
+                rule_t[:, cols(c)],
+                ALU.add,
+            )
+
+        def best(c):
+            nc.vector.tensor_reduce(
+                top[:, c[0] // D : c[1] // D],
+                cand[:, cols(c)].rearrange("p (v d) -> p v d", d=D),
+                AX,
+                ALU.max,
+            )
+
+        def add(dst, a, b, c):
+            nc.vector.tensor_tensor(dst[:, cols(c)], a[:, cols(c)], b[:, cols(c)], ALU.add)
+
+        c0, c1, c2, c3 = [(lo, lo + CHUNK) for lo in range(0, U, CHUNK)]
+        c3a, c3b = (c3[0], c3[0] + CHUNK // 2), (c3[0] + CHUNK // 2, c3[1])
+        fetch(left, la_t, c0)
+        fetch_add(c0)
+        fetch(left, la_t, c2)
+        fetch_add(c1)
+        fetch(right, ra_t, c2)
+        add(cand, part, left, c0)
+        add(part, left, rule_t, c2)
+        fetch(left, la_t, c1)
+        best(c0)
+        add(cand, part, right, c2)
+        fetch(left, la_t, c3)
+        add(cand, part, left, c1)
+        best(c2)
+        fetch(right, ra_t, c3a)
+        fetch(right, ra_t, c3b)
+        add(part, left, rule_t, c3)
+        best(c1)
+        add(cand, part, right, c3a)
+        add(cand, part, right, c3b)
+        best(c3a)
+        best(c3b)
+
+        short = sb.tile([P, W], F32, name="short")
+        nc.scalar.activation(short[:], y[:].indirect(rb_t[:]), COPY)
+        cand2 = sb.tile([P, W], F32, name="cand2")
+        top2 = sb.tile([P, W // D], F32, name="top2")
+        total = sb.tile([P, W // D], F32, name="total")
+        result = sb.tile([P, W // D], F32, name="result")
+        half = W // 2
+        for h in range(2):
+            nc.vector.tensor_tensor(
+                cand2[:, h * half : (h + 1) * half],
+                top[:].indirect(entries(lb_t, h * half, (h + 1) * half)),
+                short[:, h * half : (h + 1) * half],
+                ALU.add,
+            )
+        for h in range(2):
+            ways = cand2[:, h * half : (h + 1) * half].rearrange("p (r d) -> p r d", d=D)
+            spans = slice(h * half // D, (h + 1) * half // D)
+            nc.vector.tensor_reduce(total[:, spans], ways, AX, ALU.add)
+            nc.vector.tensor_reduce(top2[:, spans], ways, AX, ALU.max)
+        nc.vector.scalar_tensor_tensor(result[:], total[:], -0.5 / D, top2[:], ALU.mult, ALU.add)
+        nc.sync.dma_start(out, result[:])

@@ -47,12 +47,12 @@ def tile_picked_ycky_vit_p_kernel(
         rule_t = sb.tile([P, U], F32, name="rule_t")
 
         nc.vector.memset(scales[:].bitcast(I32), 0)
+        nc.sync.dma_start(w_raw[:], w1.rearrange("(o p j) m -> p o j m", o=PASSES, j=PACK))
         for q in range(4):
-            nc.gpsimd.dma_start(
+            nc.sync.dma_start(
                 scales[32 * q : 32 * q + 4 * PASSES, :].bitcast(I32),
                 x_scales[:, 4 * q : 4 * q + 4, :].bitcast(I32),
             )
-        nc.sync.dma_start(w_raw[:], w1.rearrange("(o p j) m -> p o j m", o=PASSES, j=PACK))
         nc.sync.dma_start(offs_t[:], offs)
         for o in range(PASSES):
             nc.sync.dma_start(words[o][:], x_words[o].rearrange("p n t -> p (n t)").bitcast(I32))
@@ -74,7 +74,7 @@ def tile_picked_ycky_vit_p_kernel(
 
         picked = [sb.tile([P, S], U32, name=f"picked{o}", align_bytes=64) for o in range(PASSES)]
         nc.vector.tensor_copy(picked[0][:], words[0][:].bitcast(U32).indirect(offs_t[:]))
-        picked_scales = sb.tile([P, S], U8, name="picked_scales", tag="words0", align_bytes=64)
+        picked_scales = sb.tile([P, S], U8, name="picked_scales", align_bytes=64)
         nc.vector.tensor_copy(picked_scales[:], scales[:].indirect(offs_t[:]))
 
         banks = [ps.tile([P, hi - lo], F32, name=f"bank{lo}") for lo, hi in PIECES]

@@ -138,28 +138,23 @@ def tile_picked_ycky_vit_p_kernel(
             nc.vector.tensor_tensor(dst[:, cols(c)], a[:, cols(c)], b[:, cols(c)], ALU.add)
 
         c0, c1, c2, c3 = [(lo, lo + CHUNK) for lo in range(0, U, CHUNK)]
-        c3a, c3b = (c3[0], c3[0] + CHUNK // 2), (c3[0] + CHUNK // 2, c3[1])
         fetch(left, la_t, c0)
-        fetch_add(c0)
-        fetch(left, la_t, c2)
-        fetch_add(c1)
-        fetch(right, ra_t, c2)
-        add(cand, part, left, c0)
-        add(part, left, rule_t, c2)
-        fetch(left, la_t, c1)
-        best(c0)
-        add(cand, part, right, c2)
         fetch(left, la_t, c3)
-        add(cand, part, left, c1)
-        best(c2)
-        fetch(right, ra_t, c3a)
-        fetch(right, ra_t, c3b)
+        fetch(right, ra_t, c3)
+        fetch(left, la_t, c1)
+        fetch(left, la_t, c2)
+        fetch_add(c0)
+        fetch_add(c1)
+        add(cand, part, left, c0)
         add(part, left, rule_t, c3)
+        best(c0)
+        fetch_add(c2)
+        add(cand, part, right, c3)
+        add(cand, part, left, c1)
+        best(c3)
+        add(cand, part, left, c2)
         best(c1)
-        add(cand, part, right, c3a)
-        add(cand, part, right, c3b)
-        best(c3a)
-        best(c3b)
+        best(c2)
 
         short = sb.tile([P, W], F32, name="short")
         nc.scalar.activation(short[:], y[:].indirect(rb_t[:]), COPY)

@@ -47,15 +47,24 @@ def tile_picked_ycky_vit_p_kernel(
         rule_t = sb.tile([P, U], F32, name="rule_t")
 
         nc.vector.memset(scales[:].bitcast(I32), 0)
-        nc.sync.dma_start(w_raw[:], w1.rearrange("(o p j) m -> p o j m", o=PASSES, j=PACK))
-        for q in range(4):
+        def load_scales(q, o):
             nc.sync.dma_start(
-                scales[32 * q : 32 * q + 4 * PASSES, :].bitcast(I32),
-                x_scales[:, 4 * q : 4 * q + 4, :].bitcast(I32),
+                scales[32 * q + 4 * o : 32 * q + 4 * o + 4, :].bitcast(I32),
+                x_scales[o, 4 * q : 4 * q + 4, :].bitcast(I32),
             )
-        nc.sync.dma_start(offs_t[:], offs)
-        for o in range(PASSES):
+
+        def load_words(o):
             nc.sync.dma_start(words[o][:], x_words[o].rearrange("p n t -> p (n t)").bitcast(I32))
+
+        planes = [(q, o) for q in (0, 2, 1, 3) for o in range(PASSES)]
+        nc.sync.dma_start(offs_t[:], offs)
+        nc.sync.dma_start(w_raw[:], w1.rearrange("(o p j) m -> p o j m", o=PASSES, j=PACK))
+        for q, o in planes[:3]:
+            load_scales(q, o)
+        load_words(0)
+        for q, o in planes[3:]:
+            load_scales(q, o)
+        load_words(1)
         nc.sync.dma_start(la_t[:], la)
         nc.sync.dma_start(ra_t[:], ra)
         nc.sync.dma_start(rule_t[:], rule)

from contextlib import ExitStack

import concourse.mybir as mybir

K, T, S, N, D, U, V, W = 1024, 2048, 512, 128, 4, 1024, 256, 256
FLOPS = 2 * K * N * S

F32 = mybir.dt.float32
BF16 = mybir.dt.bfloat16
I32 = mybir.dt.int32
U32 = mybir.dt.uint32
U16 = mybir.dt.uint16
U8 = mybir.dt.uint8
FP8X4 = mybir.dt.float8_e4m3fn_x4
ALU = mybir.AluOpType
COPY = mybir.ActivationFunctionType.Copy
AX = mybir.AxisListType.X

P = 128
PACK = 4
PASSES = K // (P * PACK)
PIECES = ((0, 256), (256, 384), (384, 512))
CHUNK = 256


def entries(offsets, lo, hi):
    return offsets[:, lo // 16 : hi // 16]


def tile_picked_ycky_vit_p_kernel(
    tc, x_words, x_scales, w1, rule, offs, la, ra, lb, rb, out
):
    nc = tc.nc
    with ExitStack() as ctx:
        sb = ctx.enter_context(tc.tile_pool(name="sb", bufs=1))
        ps = ctx.enter_context(tc.psum_pool(name="ps", bufs=1))

        offs_t = sb.tile([P, S // 16], U16, name="offs_t")
        la_t = sb.tile([P, U // 16], U16, name="la_t")
        ra_t = sb.tile([P, U // 16], U16, name="ra_t")
        lb_t = sb.tile([P, W // 16], U16, name="lb_t")
        rb_t = sb.tile([P, W // 16], U16, name="rb_t")

        w_raw = sb.tile([P, PASSES, PACK, N], F32, name="w_raw")
        words = [sb.tile([P, T], I32, name=f"words{o}", align_bytes=64) for o in range(PASSES)]
        scales = sb.tile([P, T], U8, name="scales")
        rule_t = sb.tile([P, U], F32, name="rule_t")

        nc.vector.memset(scales[:].bitcast(I32), 0)
        def load_scales(q, o):
            nc.sync.dma_start(
                scales[32 * q + 4 * o : 32 * q + 4 * o + 4, :].bitcast(I32),
                x_scales[o, 4 * q : 4 * q + 4, :].bitcast(I32),
            )

        def load_words(o):
            nc.sync.dma_start(words[o][:], x_words[o].rearrange("p n t -> p (n t)").bitcast(I32))

        planes = [(q, o) for q in (0, 2, 1, 3) for o in range(PASSES)]
        nc.sync.dma_start(offs_t[:], offs)
        nc.sync.dma_start(w_raw[:], w1.rearrange("(o p j) m -> p o j m", o=PASSES, j=PACK))
        for q, o in planes[:3]:
            load_scales(q, o)
        load_words(0)
        for q, o in planes[3:]:
            load_scales(q, o)
        load_words(1)
        nc.sync.dma_start(la_t[:], la)
        nc.sync.dma_start(ra_t[:], ra)
        nc.sync.dma_start(rule_t[:], rule)
        nc.sync.dma_start(rb_t[:], rb)
        nc.sync.dma_start(lb_t[:], lb)

        w_bf = sb.tile([P, PASSES, N, PACK], BF16, name="w_bf", align_bytes=64)
        nc.scalar.activation(w_bf[:], w_raw[:].rearrange("p o j m -> p o m j"), COPY)
        w_codes = sb.tile([P, PASSES * N], U32, name="w_codes", align_bytes=64)
        w_scales = sb.tile([P, PASSES * N], U8, name="w_scales", align_bytes=64)
        nc.vector.quantize_mx(
            out=w_codes[:].bitcast(FP8X4),
            scales=w_scales[:],
            in_=w_bf[:].rearrange("p o m j -> p (o m j)"),
        )

        picked = [sb.tile([P, S], U32, name=f"picked{o}", align_bytes=64) for o in range(PASSES)]
        nc.vector.tensor_copy(picked[0][:], words[0][:].bitcast(U32).indirect(offs_t[:]))
        picked_scales = sb.tile([P, S], U8, name="picked_scales", align_bytes=64)
        nc.vector.tensor_copy(picked_scales[:], scales[:].indirect(offs_t[:]))

        banks = [ps.tile([P, hi - lo], F32, name=f"bank{lo}") for lo, hi in PIECES]

        def product(bank, o, lo, hi):
            nc.tensor.matmul_mx(
                out=bank[:],
                lhsT=w_codes[:, o * N : (o + 1) * N].bitcast(FP8X4),
                lhsT_scale=w_scales[:, o * N : (o + 1) * N],
                rhs=picked[o][:, lo:hi].bitcast(FP8X4),
                rhs_scale=picked_scales[4 * o : P, lo:hi],
                start=(o == 0),
                stop=(o == PASSES - 1),
            )

        for bank, (lo, hi) in zip(banks, PIECES):
            product(bank, 0, lo, hi)
        y = sb.tile([P, S], F32, name="y")
        for lo, hi in PIECES:
            nc.vector.tensor_copy(
                picked[1][:, lo:hi], words[1][:].bitcast(U32).indirect(entries(offs_t, lo, hi))
            )
        for bank, (lo, hi) in zip(banks, PIECES):
            product(bank, 1, lo, hi)
            if hi < S:
                nc.scalar.activation(y[:, lo:hi], bank[:], COPY)
            else:
                nc.vector.tensor_copy(y[:, lo:hi], bank[:])

        left = sb.tile([P, U], F32, name="left")
        right = sb.tile([P, U], F32, name="right")
        part = sb.tile([P, U], F32, name="part")
        cand = sb.tile([P, U], F32, name="cand")
        top = sb.tile([P, V], F32, name="top")

        def cols(c):
            return slice(c[0], c[1])

        def fetch(dst, offsets, c):
            nc.scalar.activation(
                dst[:, cols(c)], y[:].indirect(entries(offsets, c[0], c[1])), COPY
            )

        def fetch_add(c):
            nc.vector.tensor_tensor(
                part[:, cols(c)],
                y[:].indirect(entries(ra_t, c[0], c[1])),
                rule_t[:, cols(c)],
                ALU.add,
            )

        def best(c):
            nc.vector.tensor_reduce(
                top[:, c[0] // D : c[1] // D],
                cand[:, cols(c)].rearrange("p (v d) -> p v d", d=D),
                AX,
                ALU.max,
            )

        def add(dst, a, b, c):
            nc.vector.tensor_tensor(dst[:, cols(c)], a[:, cols(c)], b[:, cols(c)], ALU.add)

        c0, c1, c2, c3 = [(lo, lo + CHUNK) for lo in range(0, U, CHUNK)]
        fetch(left, la_t, c0)
        fetch(left, la_t, c3)
        fetch(right, ra_t, c3)
        fetch(left, la_t, c1)
        fetch(left, la_t, c2)
        fetch_add(c0)
        fetch_add(c1)
        add(cand, part, left, c0)
        add(part, left, rule_t, c3)
        best(c0)
        fetch_add(c2)
        add(cand, part, right, c3)
        add(cand, part, left, c1)
        best(c3)
        add(cand, part, left, c2)
        best(c1)
        best(c2)

        short = sb.tile([P, W], F32, name="short")
        nc.scalar.activation(short[:], y[:].indirect(rb_t[:]), COPY)
        cand2 = sb.tile([P, W], F32, name="cand2")
        top2 = sb.tile([P, W // D], F32, name="top2")
        total = sb.tile([P, W // D], F32, name="total")
        result = sb.tile([P, W // D], F32, name="result")
        half = W // 2
        for h in range(2):
            nc.vector.tensor_tensor(
                cand2[:, h * half : (h + 1) * half],
                top[:].indirect(entries(lb_t, h * half, (h + 1) * half)),
                short[:, h * half : (h + 1) * half],
                ALU.add,
            )
        for h in range(2):
            ways = cand2[:, h * half : (h + 1) * half].rearrange("p (r d) -> p r d", d=D)
            spans = slice(h * half // D, (h + 1) * half // D)
            nc.vector.tensor_reduce(total[:, spans], ways, AX, ALU.add)
            nc.vector.tensor_reduce(top2[:, spans], ways, AX, ALU.max)
        nc.vector.scalar_tensor_tensor(result[:], total[:], -0.5 / D, top2[:], ALU.mult, ALU.add)
        nc.sync.dma_start(out, result[:])
